import numpy as np
import ml_dtypes


def mxq(x, axis, fmt="e4m3"):
    dtype, down = {"e4m3": (ml_dtypes.float8_e4m3fn, 7), "e5m2": (ml_dtypes.float8_e5m2, 14)}[fmt]
    v = np.moveaxis(np.asarray(x, np.float32).astype(ml_dtypes.bfloat16).astype(np.float64), axis, -1)
    blocks = v.reshape(v.shape[:-1] + (-1, 32))
    amax = np.abs(blocks).max(-1, keepdims=True)
    byte = np.maximum(np.where(amax > 0, np.frexp(amax)[1] - 1 + 127, 0) - down, 1)
    scale = np.exp2(byte - 127.0)
    codes = (blocks / scale).astype(np.float32).astype(dtype).astype(np.float64)
    return np.moveaxis((codes * scale).reshape(v.shape), -1, axis)


WIDE = False


def mx_kscale(k):
    if not WIDE:
        return np.ones(k)
    levels = np.array([10, -10, 5, -5, 0])
    if k % 512:
        return np.exp2(np.random.permutation(np.resize(levels, k // 32))).repeat(32)
    a = np.empty((k // 512, 16))
    for p in range(k // 512):
        a[p, :8] = np.random.permutation(np.resize(levels, 8))
        for g in range(8):
            far = levels[np.abs(levels - a[p, g]) >= 10]
            a[p, g + 8] = far[np.random.randint(len(far))]
    return np.exp2(a.ravel()).repeat(32)


def f64(x):
    return np.asarray(x).astype(np.float64)


def striped8(idx):
    return np.asarray(idx).reshape(8, -1, 16).transpose(0, 2, 1).reshape(128, -1).astype(np.uint16)


def unstriped8(offs):
    return offs.reshape(8, 16, -1).transpose(0, 2, 1).reshape(8, -1).astype(np.int64)


def pick8(x, idx, run):
    r = np.arange(len(x))
    return x[r[:, None], idx[r % (8 * run) // run]]


E2M1 = np.array([0.0, 0.5, 1.0, 1.5, 2.0, 3.0, 4.0, 6.0, -0.0, -0.5, -1.0, -1.5, -2.0, -3.0, -4.0, -6.0])


def pack_weight(w, fmt):
    k, n = w.shape
    w = f64(np.asarray(w, np.float32).astype(ml_dtypes.bfloat16)).reshape(k // 32, 32, n)
    amax = np.abs(w).max(1)
    if fmt == "e4m3":
        byte = np.frexp(amax)[1] - 1 + 127 - 7
    else:
        mant, ex = np.frexp(amax / 6.0)
        byte = np.where(mant > 0.5, ex, ex - 1) + 127
    byte = np.clip(np.where(amax > 0, byte, 1), 1, 254)
    scaled = (w * np.exp2(127.0 - byte)[:, None, :]).reshape(k, n).astype(np.float32)
    by_word = np.ascontiguousarray(scaled.reshape(k // 512, 128, 4, n).transpose(0, 1, 3, 2))
    if fmt == "e4m3":
        words = by_word.astype(ml_dtypes.float8_e4m3fn).view(np.uint8)
    else:
        c = by_word.astype(ml_dtypes.float4_e2m1fn).view(np.uint8) & 0xF
        words = (c[..., 0::2] | (c[..., 1::2] << 4)).reshape(k // 512, 128, 2 * n)
    return np.ascontiguousarray(words), np.ascontiguousarray(byte.astype(np.uint8).reshape(k // 512, 16, n))


def unpack_weight(words, scales, fmt):
    g, _, n = scales.shape
    words = np.ascontiguousarray(words).reshape(g, 128, n, -1)
    if fmt == "e4m3":
        vals = words.view(ml_dtypes.float8_e4m3fn).astype(np.float64)
    else:
        nib = np.empty((g, 128, n, 4), np.uint8)
        nib[..., 0::2] = words & 0xF
        nib[..., 1::2] = words >> 4
        vals = E2M1[nib]
    vals = vals * np.repeat(np.exp2(scales.astype(np.float64) - 127.0), 8, axis=1)[..., None]
    return vals.transpose(0, 1, 3, 2).reshape(g * 512, n)


D, T, U, I, J, Q = 512, 1024, 1024, 512, 256, 128


def setup_inputs():
    n = np.random.standard_normal
    idx = np.stack([np.random.permutation(T)[:I] for _ in range(8)])
    idx2 = np.stack([np.random.permutation(U)[:J] for _ in range(8)])
    idx3 = np.stack([np.random.permutation(U)[:I] for _ in range(8)])
    idx4 = np.stack([np.random.permutation(T)[:I] for _ in range(8)])
    idx5 = np.stack([np.random.permutation(T)[:I] for _ in range(8)])
    fd = mx_kscale(D)
    keysp = pack_weight(n((D, T)) / fd[:, None], "e4m3")
    notesp = pack_weight(n((D, U)) / fd[:, None], "e2m1")
    return {
        "query": (n((D, Q)) * 1.0 / np.sqrt(D) * fd[:, None]).astype(np.float32),
        "keys_words": keysp[0],
        "keys_scales": keysp[1],
        "notes_words": notesp[0],
        "notes_scales": notesp[1],
        "offs": striped8(idx),
        "offs2": striped8(idx2),
        "offs3": striped8(idx3),
        "offs4": striped8(idx4),
        "offs5": striped8(idx5),
    }


def reference(query, keys_words, keys_scales, notes_words, notes_scales, offs, offs2, offs3, offs4, offs5):
    idx = unstriped8(offs)
    idx2 = unstriped8(offs2)
    idx3 = unstriped8(offs3)
    idx4 = unstriped8(offs4)
    idx5 = unstriped8(offs5)
    keysu = unpack_weight(keys_words, keys_scales, "e4m3")
    notesu = unpack_weight(notes_words, notes_scales, "e2m1")
    queryq = mxq(f64(query), 0, "e4m3")
    a = queryq.T @ keysu
    b = queryq.T @ notesu
    w = pick8(a, idx, 16) * 1.25
    p2 = w.reshape(Q, J, I // J).sum(axis=2)
    f1 = np.zeros((Q, U))
    f1[np.arange(Q)[:, None], idx2[np.arange(Q) % 128 // 16]] = p2
    bb = b + f1
    v = pick8(bb, idx3, 16) - w
    f2 = np.zeros((Q, T))
    f2[np.arange(Q)[:, None], idx4[np.arange(Q) % 128 // 16]] = v
    aa = a - f2
    y = pick8(aa, idx5, 16)
    return y

@@ -1,0 +1,155 @@
+from contextlib import ExitStack
+
+import concourse.mybir as mybir
+
+D, T, U, I, J, Q = 512, 1024, 1024, 512, 256, 128
+FLOPS = 2 * D * Q * (T + U)
+
+F32 = mybir.dt.float32
+BF16 = mybir.dt.bfloat16
+I32 = mybir.dt.int32
+U32 = mybir.dt.uint32
+U16 = mybir.dt.uint16
+U8 = mybir.dt.uint8
+FP8X4 = mybir.dt.float8_e4m3fn_x4
+FP4X4 = mybir.dt.float4_e2m1fn_x4
+MULT = mybir.AluOpType.mult
+ADD = mybir.AluOpType.add
+SUB = mybir.AluOpType.subtract
+COPY = mybir.ActivationFunctionType.Copy
+
+P = 128
+PACK = 4
+BANK = 512
+A_COLS = 256
+LANES = 16
+
+
+def load_scale_rows(queue, plane, rows):
+    for quad in range(4):
+        queue.dma_start(
+            out=plane[32 * quad : 32 * quad + 4, :].bitcast(I32),
+            in_=rows[4 * quad : 4 * quad + 4, :].bitcast(I32),
+        )
+
+
+def tile_attend_pairrelay_two_kernel(
+    tc, query, keys_words, keys_scales, notes_words, notes_scales, offs, offs2, offs3, offs4, offs5, out
+):
+    nc = tc.nc
+    with ExitStack() as ctx:
+        lists = ctx.enter_context(tc.tile_pool(name="lists", bufs=1))
+        sb = ctx.enter_context(tc.tile_pool(name="sb", bufs=1))
+        psum = ctx.enter_context(tc.psum_pool(name="psum", bufs=1))
+
+        key_plane = sb.tile([P, T], U8, align_bytes=64)
+        note_plane = sb.tile([P, U], U8, align_bytes=64)
+        nc.vector.memset(key_plane[:].bitcast(I32), 0)
+
+        q_raw = sb.tile([P, PACK, Q], F32)
+        nc.sync.dma_start(out=q_raw[:], in_=query.rearrange("(p j) w -> p j w", j=PACK))
+        load_scale_rows(nc.scalar, key_plane, keys_scales[0])
+
+        key_rows = keys_words[0].rearrange("p n t -> p (n t)")
+        key_words = []
+        for half in range(T // BANK):
+            words = sb.tile([P, BANK], I32, name="key_words%d" % half, align_bytes=64)
+            nc.sync.dma_start(
+                out=words[:], in_=key_rows[:, half * BANK * PACK : (half + 1) * BANK * PACK].bitcast(I32)
+            )
+            key_words.append(words)
+
+        idx = lists.tile([P, I // LANES], U16)
+        nc.sync.dma_start(idx[:], offs)
+
+        nc.vector.memset(note_plane[:].bitcast(I32), 0)
+        note_words = sb.tile([P, 2 * U], U8, align_bytes=64)
+        nc.sync.dma_start(out=note_words[:].bitcast(I32), in_=notes_words[0].bitcast(I32))
+        idx2 = lists.tile([P, J // LANES], U16)
+        nc.sync.dma_start(idx2[:], offs2)
+        load_scale_rows(nc.sync, note_plane, notes_scales[0])
+        idx3 = lists.tile([P, I // LANES], U16)
+        nc.sync.dma_start(idx3[:], offs3)
+        idx4 = lists.tile([P, I // LANES], U16)
+        nc.sync.dma_start(idx4[:], offs4)
+        idx5 = lists.tile([P, I // LANES], U16)
+        nc.sync.dma_start(idx5[:], offs5)
+
+        f1 = sb.tile([P, U], F32)
+        f2 = sb.tile([P, T], F32)
+        nc.vector.memset(f1[:], 0.0)
+        nc.vector.memset(f2[:], 0.0)
+
+        q_grouped = sb.tile([P, Q, PACK], BF16, align_bytes=64)
+        nc.vector.tensor_copy(out=q_grouped[:], in_=q_raw[:].rearrange("p j w -> p w j"))
+        q_codes = sb.tile([P, Q], U32, align_bytes=64)
+        q_plane = sb.tile([P, Q], U8, align_bytes=64)
+        nc.vector.quantize_mx(
+            out=q_codes[:].bitcast(FP8X4), scales=q_plane[:], in_=q_grouped[:].rearrange("p w j -> p (w j)")
+        )
+
+        a = sb.tile([P, T], F32)
+        for c in range(T // A_COLS):
+            cols = slice(c * A_COLS, (c + 1) * A_COLS)
+            start = c * A_COLS % BANK
+            bank = psum.tile([P, A_COLS], F32, name="a_bank%d" % c)
+            nc.tensor.matmul_mx(
+                out=bank[:],
+                lhsT=q_codes[:].bitcast(FP8X4),
+                lhsT_scale=q_plane[:],
+                rhs=key_words[c * A_COLS // BANK][:, start : start + A_COLS].bitcast(FP8X4),
+                rhs_scale=key_plane[:, cols],
+                start=True,
+                stop=True,
+            )
+            if c % 2 == 0:
+                nc.scalar.copy(out=a[:, cols], in_=bank[:])
+            else:
+                nc.vector.tensor_copy(out=a[:, cols], in_=bank[:])
+
+        b_banks = []
+        for c in range(U // BANK):
+            bank = psum.tile([P, BANK], F32, name="b_bank%d" % c)
+            nc.tensor.matmul_mx(
+                out=bank[:],
+                lhsT=q_codes[:].bitcast(FP8X4),
+                lhsT_scale=q_plane[:],
+                rhs=note_words[:, 2 * c * BANK : 2 * (c + 1) * BANK].bitcast(FP4X4),
+                rhs_scale=note_plane[:, c * BANK : (c + 1) * BANK],
+                start=True,
+                stop=True,
+            )
+            b_banks.append(bank)
+
+        half = I // 2
+        cut = half // LANES
+
+        w = sb.tile([P, I], F32)
+        nc.vector.tensor_scalar(w[:, :half], a[:].indirect(idx[:, :cut]), 1.25, 0.0, MULT, ADD)
+        nc.scalar.activation(w[:, half:], a[:].indirect(idx[:, cut:]), COPY, scale=1.25)
+
+        p2 = sb.tile([P, J], F32)
+        nc.vector.tensor_tensor(p2[:], w[:, 0::2], w[:, 1::2], ADD)
+        nc.vector.tensor_copy(f1[:].indirect(idx2[:]), p2[:])
+        minus_w = sb.tile([P, I], F32)
+        nc.scalar.activation(minus_w[:], w[:], COPY, scale=-1.0)
+
+        bb = sb.tile([P, U], F32)
+        for c in range(U // BANK):
+            cols = slice(c * BANK, (c + 1) * BANK)
+            nc.vector.tensor_tensor(bb[:, cols], b_banks[c][:], f1[:, cols], ADD)
+
+        picked = sb.tile([P, I], F32)
+        nc.vector.tensor_copy(picked[:, :half], bb[:].indirect(idx3[:, :cut]))
+        nc.scalar.activation(picked[:, half:], bb[:].indirect(idx3[:, cut:]), COPY)
+        nc.vector.tensor_tensor(f2[:].indirect(idx4[:]), picked[:], minus_w[:], ADD)
+
+        aa = sb.tile([P, T], F32)
+        nc.vector.tensor_tensor(aa[:], a[:], f2[:], SUB)
+
+        y0 = sb.tile([P, half], F32)
+        y1 = sb.tile([P, half], F32)
+        nc.vector.tensor_copy(y0[:], aa[:].indirect(idx5[:, :cut]))
+        nc.scalar.activation(y1[:], aa[:].indirect(idx5[:, cut:]), COPY)
+        nc.sync.dma_start(out=out[:, :half], in_=y0[:])
+        nc.scalar.dma_start(out=out[:, half:], in_=y1[:])

@@ -21,7 +21,8 @@ COPY = mybir.ActivationFunctionType.Copy
 P = 128
 PACK = 4
 BANK = 512
-A_COLS = 256
+A_WIDTHS = (512, 256, 128, 128)
+SPLIT = 704
 LANES = 16
 
 
@@ -76,36 +77,44 @@ def tile_attend_pairrelay_two_kernel(
         nc.sync.dma_start(idx5[:], offs5)
 
         f1 = sb.tile([P, U], F32)
-        f2 = sb.tile([P, T], F32)
         nc.vector.memset(f1[:], 0.0)
-        nc.vector.memset(f2[:], 0.0)
 
-        q_grouped = sb.tile([P, Q, PACK], BF16, align_bytes=64)
-        nc.vector.tensor_copy(out=q_grouped[:], in_=q_raw[:].rearrange("p j w -> p w j"))
+        q_grouped = sb.tile([P, Q, PACK], BF16, align_bytes=64, tag="shared")
+        nc.vector.tensor_copy(
+            out=q_grouped[:].rearrange("p (c i) j -> p c j i", i=4),
+            in_=q_raw[:].rearrange("p j (c i) -> p c j i", i=4),
+        )
         q_codes = sb.tile([P, Q], U32, align_bytes=64)
         q_plane = sb.tile([P, Q], U8, align_bytes=64)
         nc.vector.quantize_mx(
             out=q_codes[:].bitcast(FP8X4), scales=q_plane[:], in_=q_grouped[:].rearrange("p w j -> p (w j)")
         )
 
+        f2 = sb.tile([P, T], F32, align_bytes=64, tag="shared")
+        nc.vector.memset(f2[:], 0.0)
+
         a = sb.tile([P, T], F32)
-        for c in range(T // A_COLS):
-            cols = slice(c * A_COLS, (c + 1) * A_COLS)
-            start = c * A_COLS % BANK
-            bank = psum.tile([P, A_COLS], F32, name="a_bank%d" % c)
+        a_banks = []
+        first = 0
+        for c, width in enumerate(A_WIDTHS):
+            cols = slice(first, first + width)
+            start = first % BANK
+            bank = psum.tile([P, width], F32, name="a_bank%d" % c)
             nc.tensor.matmul_mx(
                 out=bank[:],
                 lhsT=q_codes[:].bitcast(FP8X4),
                 lhsT_scale=q_plane[:],
-                rhs=key_words[c * A_COLS // BANK][:, start : start + A_COLS].bitcast(FP8X4),
+                rhs=key_words[first // BANK][:, start : start + width].bitcast(FP8X4),
                 rhs_scale=key_plane[:, cols],
                 start=True,
                 stop=True,
             )
-            if c % 2 == 0:
+            if c in (0, 3):
                 nc.scalar.copy(out=a[:, cols], in_=bank[:])
             else:
                 nc.vector.tensor_copy(out=a[:, cols], in_=bank[:])
+            a_banks.append(bank)
+            first += width
 
         b_banks = []
         for c in range(U // BANK):
@@ -131,13 +140,15 @@ def tile_attend_pairrelay_two_kernel(
         p2 = sb.tile([P, J], F32)
         nc.vector.tensor_tensor(p2[:], w[:, 0::2], w[:, 1::2], ADD)
         nc.vector.tensor_copy(f1[:].indirect(idx2[:]), p2[:])
+        b_tail = sb.tile([P, U - SPLIT], F32)
+        nc.scalar.copy(out=b_tail[:], in_=b_banks[1][:, SPLIT - BANK :])
         minus_w = sb.tile([P, I], F32)
         nc.scalar.activation(minus_w[:], w[:], COPY, scale=-1.0)
 
         bb = sb.tile([P, U], F32)
-        for c in range(U // BANK):
-            cols = slice(c * BANK, (c + 1) * BANK)
-            nc.vector.tensor_tensor(bb[:, cols], b_banks[c][:], f1[:, cols], ADD)
+        nc.vector.tensor_tensor(bb[:, :BANK], b_banks[0][:], f1[:, :BANK], ADD)
+        nc.vector.tensor_tensor(bb[:, BANK:SPLIT], b_banks[1][:, : SPLIT - BANK], f1[:, BANK:SPLIT], ADD)
+        nc.gpsimd.tensor_tensor(bb[:, SPLIT:], b_tail[:], f1[:, SPLIT:], ADD)
 
         picked = sb.tile([P, I], F32)
         nc.vector.tensor_copy(picked[:, :half], bb[:].indirect(idx3[:, :cut]))
@@ -145,7 +156,9 @@ def tile_attend_pairrelay_two_kernel(
         nc.vector.tensor_tensor(f2[:].indirect(idx4[:]), picked[:], minus_w[:], ADD)
 
         aa = sb.tile([P, T], F32)
-        nc.vector.tensor_tensor(aa[:], a[:], f2[:], SUB)
+        nc.vector.tensor_tensor(aa[:, :BANK], a_banks[0][:], f2[:, :BANK], SUB)
+        nc.vector.tensor_tensor(aa[:, BANK:SPLIT], a_banks[1][:, : SPLIT - BANK], f2[:, BANK:SPLIT], SUB)
+        nc.gpsimd.tensor_tensor(aa[:, SPLIT:], a[:, SPLIT:], f2[:, SPLIT:], SUB)
 
         y0 = sb.tile([P, half], F32)
         y1 = sb.tile([P, half], F32)

@@ -26,9 +26,9 @@ SPLIT = 704
 LANES = 16
 
 
-def load_scale_rows(queue, plane, rows):
+def load_scale_rows(queues, plane, rows):
     for quad in range(4):
-        queue.dma_start(
+        queues[quad].dma_start(
             out=plane[32 * quad : 32 * quad + 4, :].bitcast(I32),
             in_=rows[4 * quad : 4 * quad + 4, :].bitcast(I32),
         )
@@ -49,7 +49,8 @@ def tile_attend_pairrelay_two_kernel(
 
         q_raw = sb.tile([P, PACK, Q], F32)
         nc.sync.dma_start(out=q_raw[:], in_=query.rearrange("(p j) w -> p j w", j=PACK))
-        load_scale_rows(nc.scalar, key_plane, keys_scales[0])
+        idx = lists.tile([P, I // LANES], U16)
+        nc.sync.dma_start(idx[:], offs)
 
         key_rows = keys_words[0].rearrange("p n t -> p (n t)")
         key_words = []
@@ -59,16 +60,15 @@ def tile_attend_pairrelay_two_kernel(
                 out=words[:], in_=key_rows[:, half * BANK * PACK : (half + 1) * BANK * PACK].bitcast(I32)
             )
             key_words.append(words)
-
-        idx = lists.tile([P, I // LANES], U16)
-        nc.sync.dma_start(idx[:], offs)
+            if half == 0:
+                load_scale_rows((nc.scalar, nc.sync, nc.scalar, nc.sync), key_plane, keys_scales[0])
 
         nc.vector.memset(note_plane[:].bitcast(I32), 0)
         note_words = sb.tile([P, 2 * U], U8, align_bytes=64)
         nc.sync.dma_start(out=note_words[:].bitcast(I32), in_=notes_words[0].bitcast(I32))
         idx2 = lists.tile([P, J // LANES], U16)
         nc.sync.dma_start(idx2[:], offs2)
-        load_scale_rows(nc.sync, note_plane, notes_scales[0])
+        load_scale_rows((nc.sync,) * 4, note_plane, notes_scales[0])
         idx3 = lists.tile([P, I // LANES], U16)
         nc.sync.dma_start(idx3[:], offs3)
         idx4 = lists.tile([P, I // LANES], U16)

from contextlib import ExitStack

import concourse.mybir as mybir

D, T, U, I, J, Q = 512, 1024, 1024, 512, 256, 128
FLOPS = 2 * D * Q * (T + U)

F32 = mybir.dt.float32
BF16 = mybir.dt.bfloat16
I32 = mybir.dt.int32
U32 = mybir.dt.uint32
U16 = mybir.dt.uint16
U8 = mybir.dt.uint8
FP8X4 = mybir.dt.float8_e4m3fn_x4
FP4X4 = mybir.dt.float4_e2m1fn_x4
MULT = mybir.AluOpType.mult
ADD = mybir.AluOpType.add
SUB = mybir.AluOpType.subtract
COPY = mybir.ActivationFunctionType.Copy

P = 128
PACK = 4
BANK = 512
A_WIDTHS = (512, 256, 128, 128)
SPLIT = 704
LANES = 16


def load_scale_rows(queues, plane, rows):
    for quad in range(4):
        queues[quad].dma_start(
            out=plane[32 * quad : 32 * quad + 4, :].bitcast(I32),
            in_=rows[4 * quad : 4 * quad + 4, :].bitcast(I32),
        )


def tile_attend_pairrelay_two_kernel(
    tc, query, keys_words, keys_scales, notes_words, notes_scales, offs, offs2, offs3, offs4, offs5, out
):
    nc = tc.nc
    with ExitStack() as ctx:
        lists = ctx.enter_context(tc.tile_pool(name="lists", bufs=1))
        sb = ctx.enter_context(tc.tile_pool(name="sb", bufs=1))
        psum = ctx.enter_context(tc.psum_pool(name="psum", bufs=1))

        key_plane = sb.tile([P, T], U8, align_bytes=64)
        note_plane = sb.tile([P, U], U8, align_bytes=64)
        nc.vector.memset(key_plane[:].bitcast(I32), 0)

        q_raw = sb.tile([P, PACK, Q], F32)
        nc.sync.dma_start(out=q_raw[:], in_=query.rearrange("(p j) w -> p j w", j=PACK))
        idx = lists.tile([P, I // LANES], U16)
        nc.sync.dma_start(idx[:], offs)

        key_rows = keys_words[0].rearrange("p n t -> p (n t)")
        key_words = []
        for half in range(T // BANK):
            words = sb.tile([P, BANK], I32, name="key_words%d" % half, align_bytes=64)
            nc.sync.dma_start(
                out=words[:], in_=key_rows[:, half * BANK * PACK : (half + 1) * BANK * PACK].bitcast(I32)
            )
            key_words.append(words)
            if half == 0:
                load_scale_rows((nc.scalar, nc.sync, nc.scalar, nc.sync), key_plane, keys_scales[0])

        nc.vector.memset(note_plane[:].bitcast(I32), 0)
        note_words = sb.tile([P, 2 * U], U8, align_bytes=64)
        nc.sync.dma_start(out=note_words[:].bitcast(I32), in_=notes_words[0].bitcast(I32))
        idx2 = lists.tile([P, J // LANES], U16)
        nc.sync.dma_start(idx2[:], offs2)
        load_scale_rows((nc.sync,) * 4, note_plane, notes_scales[0])
        idx3 = lists.tile([P, I // LANES], U16)
        nc.sync.dma_start(idx3[:], offs3)
        idx4 = lists.tile([P, I // LANES], U16)
        nc.sync.dma_start(idx4[:], offs4)
        idx5 = lists.tile([P, I // LANES], U16)
        nc.sync.dma_start(idx5[:], offs5)

        f1 = sb.tile([P, U], F32)
        nc.vector.memset(f1[:], 0.0)

        q_grouped = sb.tile([P, Q, PACK], BF16, align_bytes=64, tag="shared")
        nc.vector.tensor_copy(
            out=q_grouped[:].rearrange("p (c i) j -> p c j i", i=4),
            in_=q_raw[:].rearrange("p j (c i) -> p c j i", i=4),
        )
        q_codes = sb.tile([P, Q], U32, align_bytes=64)
        q_plane = sb.tile([P, Q], U8, align_bytes=64)
        nc.vector.quantize_mx(
            out=q_codes[:].bitcast(FP8X4), scales=q_plane[:], in_=q_grouped[:].rearrange("p w j -> p (w j)")
        )

        f2 = sb.tile([P, T], F32, align_bytes=64, tag="shared")
        nc.vector.memset(f2[:], 0.0)

        a = sb.tile([P, T], F32)
        a_banks = []
        first = 0
        for c, width in enumerate(A_WIDTHS):
            cols = slice(first, first + width)
            start = first % BANK
            bank = psum.tile([P, width], F32, name="a_bank%d" % c)
            nc.tensor.matmul_mx(
                out=bank[:],
                lhsT=q_codes[:].bitcast(FP8X4),
                lhsT_scale=q_plane[:],
                rhs=key_words[first // BANK][:, start : start + width].bitcast(FP8X4),
                rhs_scale=key_plane[:, cols],
                start=True,
                stop=True,
            )
            if c in (0, 3):
                nc.scalar.copy(out=a[:, cols], in_=bank[:])
            else:
                nc.vector.tensor_copy(out=a[:, cols], in_=bank[:])
            a_banks.append(bank)
            first += width

        b_banks = []
        for c in range(U // BANK):
            bank = psum.tile([P, BANK], F32, name="b_bank%d" % c)
            nc.tensor.matmul_mx(
                out=bank[:],
                lhsT=q_codes[:].bitcast(FP8X4),
                lhsT_scale=q_plane[:],
                rhs=note_words[:, 2 * c * BANK : 2 * (c + 1) * BANK].bitcast(FP4X4),
                rhs_scale=note_plane[:, c * BANK : (c + 1) * BANK],
                start=True,
                stop=True,
            )
            b_banks.append(bank)

        half = I // 2
        cut = half // LANES

        w = sb.tile([P, I], F32)
        nc.vector.tensor_scalar(w[:, :half], a[:].indirect(idx[:, :cut]), 1.25, 0.0, MULT, ADD)
        nc.scalar.activation(w[:, half:], a[:].indirect(idx[:, cut:]), COPY, scale=1.25)

        p2 = sb.tile([P, J], F32)
        nc.vector.tensor_tensor(p2[:], w[:, 0::2], w[:, 1::2], ADD)
        nc.vector.tensor_copy(f1[:].indirect(idx2[:]), p2[:])
        b_tail = sb.tile([P, U - SPLIT], F32)
        nc.scalar.copy(out=b_tail[:], in_=b_banks[1][:, SPLIT - BANK :])
        minus_w = sb.tile([P, I], F32)
        nc.scalar.activation(minus_w[:], w[:], COPY, scale=-1.0)

        bb = sb.tile([P, U], F32)
        nc.vector.tensor_tensor(bb[:, :BANK], b_banks[0][:], f1[:, :BANK], ADD)
        nc.vector.tensor_tensor(bb[:, BANK:SPLIT], b_banks[1][:, : SPLIT - BANK], f1[:, BANK:SPLIT], ADD)
        nc.gpsimd.tensor_tensor(bb[:, SPLIT:], b_tail[:], f1[:, SPLIT:], ADD)

        picked = sb.tile([P, I], F32)
        nc.vector.tensor_copy(picked[:, :half], bb[:].indirect(idx3[:, :cut]))
        nc.scalar.activation(picked[:, half:], bb[:].indirect(idx3[:, cut:]), COPY)
        nc.vector.tensor_tensor(f2[:].indirect(idx4[:]), picked[:], minus_w[:], ADD)

        aa = sb.tile([P, T], F32)
        nc.vector.tensor_tensor(aa[:, :BANK], a_banks[0][:], f2[:, :BANK], SUB)
        nc.vector.tensor_tensor(aa[:, BANK:SPLIT], a_banks[1][:, : SPLIT - BANK], f2[:, BANK:SPLIT], SUB)
        nc.gpsimd.tensor_tensor(aa[:, SPLIT:], a[:, SPLIT:], f2[:, SPLIT:], SUB)

        y0 = sb.tile([P, half], F32)
        y1 = sb.tile([P, half], F32)
        nc.vector.tensor_copy(y0[:], aa[:].indirect(idx5[:, :cut]))
        nc.scalar.activation(y1[:], aa[:].indirect(idx5[:, cut:]), COPY)
        nc.sync.dma_start(out=out[:, :half], in_=y0[:])
        nc.scalar.dma_start(out=out[:, half:], in_=y1[:])
